import numpy as np
import ml_dtypes


def mxq(x, axis, fmt="e4m3"):
    dtype, down = {"e4m3": (ml_dtypes.float8_e4m3fn, 7), "e5m2": (ml_dtypes.float8_e5m2, 14)}[fmt]
    v = np.moveaxis(np.asarray(x, np.float32).astype(ml_dtypes.bfloat16).astype(np.float64), axis, -1)
    blocks = v.reshape(v.shape[:-1] + (-1, 32))
    amax = np.abs(blocks).max(-1, keepdims=True)
    byte = np.maximum(np.where(amax > 0, np.frexp(amax)[1] - 1 + 127, 0) - down, 1)
    scale = np.exp2(byte - 127.0)
    codes = (blocks / scale).astype(np.float32).astype(dtype).astype(np.float64)
    return np.moveaxis((codes * scale).reshape(v.shape), -1, axis)


WIDE = False


def mx_kscale(k):
    if not WIDE:
        return np.ones(k)
    levels = np.array([10, -10, 5, -5, 0])
    if k % 512:
        return np.exp2(np.random.permutation(np.resize(levels, k // 32))).repeat(32)
    a = np.empty((k // 512, 16))
    for p in range(k // 512):
        a[p, :8] = np.random.permutation(np.resize(levels, 8))
        for g in range(8):
            far = levels[np.abs(levels - a[p, g]) >= 10]
            a[p, g + 8] = far[np.random.randint(len(far))]
    return np.exp2(a.ravel()).repeat(32)


def f64(x):
    return np.asarray(x).astype(np.float64)


def striped(idx):
    return np.tile(np.asarray(idx).reshape(-1, 16).T, (8, 1)).astype(np.uint16)


def unstriped(offs):
    return offs[:16].T.reshape(-1).astype(np.int64)


E2M1 = np.array([0.0, 0.5, 1.0, 1.5, 2.0, 3.0, 4.0, 6.0, -0.0, -0.5, -1.0, -1.5, -2.0, -3.0, -4.0, -6.0])


def pack_weight(w, fmt):
    k, n = w.shape
    w = f64(np.asarray(w, np.float32).astype(ml_dtypes.bfloat16)).reshape(k // 32, 32, n)
    amax = np.abs(w).max(1)
    if fmt == "e4m3":
        byte = np.frexp(amax)[1] - 1 + 127 - 7
    else:
        mant, ex = np.frexp(amax / 6.0)
        byte = np.where(mant > 0.5, ex, ex - 1) + 127
    byte = np.clip(np.where(amax > 0, byte, 1), 1, 254)
    scaled = (w * np.exp2(127.0 - byte)[:, None, :]).reshape(k, n).astype(np.float32)
    by_word = np.ascontiguousarray(scaled.reshape(k // 512, 128, 4, n).transpose(0, 1, 3, 2))
    if fmt == "e4m3":
        words = by_word.astype(ml_dtypes.float8_e4m3fn).view(np.uint8)
    else:
        c = by_word.astype(ml_dtypes.float4_e2m1fn).view(np.uint8) & 0xF
        words = (c[..., 0::2] | (c[..., 1::2] << 4)).reshape(k // 512, 128, 2 * n)
    return np.ascontiguousarray(words), np.ascontiguousarray(byte.astype(np.uint8).reshape(k // 512, 16, n))


def unpack_weight(words, scales, fmt):
    g, _, n = scales.shape
    words = np.ascontiguousarray(words).reshape(g, 128, n, -1)
    if fmt == "e4m3":
        vals = words.view(ml_dtypes.float8_e4m3fn).astype(np.float64)
    else:
        nib = np.empty((g, 128, n, 4), np.uint8)
        nib[..., 0::2] = words & 0xF
        nib[..., 1::2] = words >> 4
        vals = E2M1[nib]
    vals = vals * np.repeat(np.exp2(scales.astype(np.float64) - 127.0), 8, axis=1)[..., None]
    return vals.transpose(0, 1, 3, 2).reshape(g * 512, n)


def bf(x):
    return np.asarray(x, np.float32).astype(ml_dtypes.bfloat16)


def planes(Y):
    r, m = Y.shape
    b = f64(bf(Y)).reshape(r // 32, 32, m)
    amax = np.abs(b).max(1)
    byte = np.clip(np.where(amax > 0, np.frexp(amax)[1] - 1 + 127 - 7, 1), 1, 254)
    codes = (b * np.exp2(127.0 - byte)[:, None, :]).reshape(r, m).astype(np.float32).astype(ml_dtypes.float8_e4m3fn).view(np.uint8)
    words = codes.reshape(r // 512, 128, 4, m).transpose(0, 1, 3, 2)
    return np.ascontiguousarray(words), np.ascontiguousarray(byte.astype(np.uint8).reshape(r // 512, 16, m))


D, E, T, I, Q, G = 512, 512, 2048, 512, 512, 64


def setup_inputs():
    n = np.random.standard_normal
    idx = np.random.permutation(T)[:I]
    fd = mx_kscale(D)
    fe = mx_kscale(E)
    keysp = pack_weight(n((D, T)) / fd[:, None], "e2m1")
    valsp = pack_weight(n((E, T)) / fe[:, None], "e2m1")
    return {
        "query": (n((D, Q)) * 0.5 / np.sqrt(D) * fd[:, None]).astype(np.float32),
        "keys_words": keysp[0],
        "keys_scales": keysp[1],
        "sharp": (np.random.uniform(0.5, 2.0, (I, 1))).astype(np.float32),
        "lse": (np.random.uniform(6.2, 6.5, (1, Q))).astype(np.float32),
        "gout": (n((E, Q)) * 1 / np.sqrt(E) * fe[:, None]).astype(np.float32),
        "vals_words": valsp[0],
        "vals_scales": valsp[1],
        "delta": (np.random.uniform(-0.3, 0.3, (1, Q))).astype(np.float32),
        "old": (1.0 * n((I, G))).astype(np.float32),
        "offs": striped(idx),
    }


def reference(query, keys_words, keys_scales, sharp, lse, gout, vals_words, vals_scales, delta, old, offs):
    idx = unstriped(offs)
    keysu = unpack_weight(keys_words, keys_scales, "e2m1")
    valsu = unpack_weight(vals_words, vals_scales, "e2m1")
    keysidxg = keysu[:, idx]
    queryq = mxq(f64(query), 0, "e4m3")
    a = keysidxg.T @ queryq
    valsidxg = valsu[:, idx]
    goutq = mxq(f64(gout), 0, "e4m3")
    dp = valsidxg.T @ goutq
    ds = np.exp(a * f64(sharp) - f64(lse)) * (dp - f64(delta)) * a * 512.0
    y = ds.reshape(I, G, Q // G).sum(axis=2) + f64(old)
    words, scales = planes(y)
    return y, words, scales

@@ -1,0 +1,168 @@
+from contextlib import ExitStack
+
+import concourse.mybir as mybir
+from concourse.masks import make_identity
+
+D, E, T, I, Q, G = 512, 512, 2048, 512, 512, 64
+FLOPS = 2 * I * Q * (D + E)
+
+F32 = mybir.dt.float32
+BF16 = mybir.dt.bfloat16
+I32 = mybir.dt.int32
+U32 = mybir.dt.uint32
+U16 = mybir.dt.uint16
+U8 = mybir.dt.uint8
+FP8X4 = mybir.dt.float8_e4m3fn_x4
+FP4X4 = mybir.dt.float4_e2m1fn_x4
+ALU = mybir.AluOpType
+ACT = mybir.ActivationFunctionType
+
+P = 128
+PACK = 4
+HALVES = 2
+SCALE = 512.0
+
+
+def tile_attend_gsharpness_pl_kernel(tc, query, keys_words, keys_scales, sharp, lse, gout, vals_words,
+                                      vals_scales, delta, old, offs, out_0, out_1, out_2):
+    nc = tc.nc
+    with ExitStack() as ctx:
+        keep = ctx.enter_context(tc.tile_pool(name="keep", bufs=1))
+        psum = ctx.enter_context(tc.psum_pool(name="psum", bufs=1))
+
+        def sb(name, shape, dtype):
+            return keep.tile(shape, dtype, name=name, align_bytes=64)
+
+        offsets = sb("offsets", [P, I // 16], U16)
+        key_words = sb("key_words", [P, T], U16)
+        val_words = sb("val_words", [P, T], U16)
+        key_bytes = sb("key_bytes", [P, T], U8)
+        val_bytes = sb("val_bytes", [P, T], U8)
+        width = Q // HALVES
+        q_raw = [sb("q_raw%d" % c, [P, PACK, width], F32) for c in range(HALVES)]
+        g_raw = [sb("g_raw%d" % c, [P, PACK, width], F32) for c in range(HALVES)]
+        sharp_col = sb("sharp_col", [P, PACK], F32)
+        lse_col = sb("lse_col", [P, PACK], F32)
+        delta_col = sb("delta_col", [P, PACK], F32)
+        old_sb = sb("old_sb", [P, PACK, G], F32)
+        ident = sb("ident", [P, P], F32)
+
+        nc.vector.memset(key_bytes[:].bitcast(I32), 0)
+        nc.vector.memset(val_bytes[:].bitcast(I32), 0)
+
+        def load_rows(dst, src, c):
+            nc.sync.dma_start(out=dst[c][:], in_=src.rearrange("(p j) q -> p j q", j=PACK)[:, :, c * width:(c + 1) * width])
+
+        def load_scales(queue, dst, src):
+            for quad in range(4):
+                queue.dma_start(out=dst[32 * quad:32 * quad + 4, :].bitcast(I32),
+                                in_=src[0, 4 * quad:4 * quad + 4, :].bitcast(I32))
+
+        make_identity(nc, ident[:])
+        nc.sync.dma_start(offsets[:], offs)
+        nc.sync.dma_start(out=key_words[:].bitcast(I32), in_=keys_words[0].bitcast(I32))
+        load_scales(nc.sync, key_bytes, keys_scales)
+        load_rows(q_raw, query, 0)
+        load_rows(q_raw, query, 1)
+        load_scales(nc.sync, val_bytes, vals_scales)
+        nc.sync.dma_start(out=sharp_col[:], in_=sharp.rearrange("(p r) o -> p (r o)", r=PACK))
+        nc.sync.dma_start(out=val_words[:].bitcast(I32), in_=vals_words[0].bitcast(I32))
+        nc.sync.dma_start(out=lse_col[:], in_=lse.rearrange("o (p m) -> (o p) m", m=PACK))
+        load_rows(g_raw, gout, 0)
+        load_rows(g_raw, gout, 1)
+        nc.sync.dma_start(out=delta_col[:], in_=delta.rearrange("o (p m) -> (o p) m", m=PACK))
+        nc.sync.dma_start(out=old_sb[:], in_=old.rearrange("(p r) g -> p r g", r=PACK))
+
+        def gather(name, window, dtype):
+            picked = sb(name, [P, I], dtype)
+            nc.vector.tensor_copy(picked[:], window[:].indirect(offsets[:]))
+            return picked
+
+        def round_rows(name, raw):
+            grouped = sb(name, [P, PACK, P, PACK], BF16)
+            per = P // HALVES
+            for c in range(HALVES):
+                nc.scalar.copy(out=grouped[:, :, c * per:(c + 1) * per, :].rearrange("p m s j -> p s m j"),
+                               in_=raw[c][:].rearrange("p j (s m) -> p s m j", m=PACK))
+            return grouped
+
+        def quantize(name, grouped):
+            codes = sb(name + "_codes", [P, Q], U32)
+            scales = sb(name + "_scales", [P, Q], U8)
+            flat = grouped[:].rearrange("p m s j -> p (m s j)")
+            for c in range(2):
+                cols = slice(c * 256, (c + 1) * 256)
+                nc.vector.quantize_mx(out=codes[:, cols].bitcast(FP8X4), scales=scales[:, cols],
+                                      in_=flat[:, c * 1024:(c + 1) * 1024])
+            return codes, scales
+
+        def product(name, rows, words, bytes_, m):
+            codes, scales = rows
+            bank = psum.tile([P, I], F32, name=name, tag="product", bufs=7)
+            cols = slice(m * P, (m + 1) * P)
+            nc.tensor.matmul_mx(out=bank[:], lhsT=codes[:, cols].bitcast(FP8X4), lhsT_scale=scales[:, cols],
+                                rhs=words[:].bitcast(FP4X4), rhs_scale=bytes_[:], start=True, stop=True)
+            return bank[:].rearrange("p (s r) -> p r s", r=PACK)
+
+        q_bf = round_rows("q_bf", q_raw)
+        k_words = gather("k_words", key_words, U16)
+        k_bytes = gather("k_bytes", key_bytes, U8)
+        v_bytes = gather("v_bytes", val_bytes, U8)
+        q_mx = quantize("q", q_bf)
+
+        neg_lse = sb("neg_lse", [P, PACK], F32)
+        nc.scalar.activation(out=neg_lse[:], in_=lse_col[:], func=ACT.Copy, scale=-1.0)
+        spread = psum.tile([P, PACK, P], F32, name="spread", tag="turned", bufs=1)
+        for r in range(PACK):
+            nc.tensor.transpose(spread[:, r, :], sharp_col[:, r:r + 1].to_broadcast([P, P]), ident[:])
+        sharp_row = sb("sharp_row", [P, PACK, P], F32)
+        nc.scalar.copy(out=sharp_row[:], in_=spread[:])
+
+        scores = [product("a%d" % m, q_mx, k_words, k_bytes, m) for m in range(PACK)]
+        v_words = gather("v_words", val_words, U16)
+        g_bf = round_rows("g_bf", g_raw)
+
+        weights = []
+        for m in range(PACK):
+            logit = sb("logit%d" % m, [P, PACK, P], F32)
+            nc.vector.tensor_tensor(out=logit[:], in0=scores[m], in1=sharp_row[:], op=ALU.mult)
+            weight = sb("weight%d" % m, [P, PACK, P], F32)
+            nc.scalar.activation(out=weight[:], in_=logit[:], func=ACT.Exp, bias=neg_lse[:, m:m + 1])
+            weights.append(weight)
+
+        g_mx = quantize("g", g_bf)
+        scored = []
+        for m in range(PACK):
+            both = sb("both%d" % m, [P, PACK, P], F32)
+            nc.vector.scalar_tensor_tensor(out=both[:], in0=scores[m], scalar=SCALE, in1=weights[m][:],
+                                           op0=ALU.mult, op1=ALU.mult)
+            scored.append(both)
+
+        summed = psum.tile([P, PACK, P], F32, name="summed", tag="turned", bufs=1)
+        for m in range(PACK):
+            grad = product("dp%d" % m, g_mx, v_words, v_bytes, m)
+            ds = sb("ds%d" % m, [P, PACK, P], F32)
+            nc.vector.scalar_tensor_tensor(out=ds[:], in0=grad, scalar=delta_col[:, m:m + 1], in1=scored[m][:],
+                                           op0=ALU.subtract, op1=ALU.mult)
+            for r in range(PACK):
+                nc.tensor.matmul(summed[:, r, :], lhsT=ds[:, r, :], rhs=ident[:], is_transpose=True,
+                                 start=(m == 0 and r == 0), stop=(m == PACK - 1 and r == PACK - 1))
+
+        pairs = summed[:].rearrange("p r (g h) -> p h r g", h=2)
+        partial = sb("partial", [P, PACK, G], F32)
+        nc.vector.tensor_tensor(out=partial[:], in0=pairs[:, 0], in1=old_sb[:], op=ALU.add)
+        result = sb("result", [P, PACK, G], F32)
+        nc.vector.tensor_tensor(out=result[:], in0=pairs[:, 1], in1=partial[:], op=ALU.add)
+        nc.sync.dma_start(out=out_0.rearrange("(p r) g -> p r g", r=PACK), in_=result[:])
+
+        rounded = sb("rounded", [P, G, PACK], BF16)
+        nc.vector.tensor_copy(out=rounded[:], in_=result[:].rearrange("p r g -> p g r"))
+        out_codes = sb("out_codes", [P, G], U32)
+        out_scales = sb("out_scales", [P, G], U8)
+        nc.vector.quantize_mx(out=out_codes[:].bitcast(FP8X4), scales=out_scales[:],
+                              in_=rounded[:].rearrange("p g r -> p (g r)"))
+        nc.sync.dma_start(out=out_1[0].rearrange("p c t -> p (c t)").bitcast(I32), in_=out_codes[:].bitcast(I32))
+        for quad in range(4):
+            queue = nc.scalar if quad % 2 == 0 else nc.sync
+            queue.dma_start(out=out_2[0, 4 * quad:4 * quad + 4, :].bitcast(I32),
+                            in_=out_scales[32 * quad:32 * quad + 4, :].bitcast(I32))

@@ -54,17 +54,16 @@ def tile_attend_gsharpness_pl_kernel(tc, query, keys_words, keys_scales, sharp, 
             nc.sync.dma_start(out=dst[c][:], in_=src.rearrange("(p j) q -> p j q", j=PACK)[:, :, c * width:(c + 1) * width])
 
         def load_scales(queue, dst, src):
-            for quad in range(4):
-                queue.dma_start(out=dst[32 * quad:32 * quad + 4, :].bitcast(I32),
-                                in_=src[0, 4 * quad:4 * quad + 4, :].bitcast(I32))
+            for row in range(4):
+                queue.dma_start(out=dst[row:P:32, :].bitcast(I32), in_=src[0, row:16:4, :].bitcast(I32))
 
         make_identity(nc, ident[:])
         nc.sync.dma_start(offsets[:], offs)
         nc.sync.dma_start(out=key_words[:].bitcast(I32), in_=keys_words[0].bitcast(I32))
         load_scales(nc.sync, key_bytes, keys_scales)
         load_rows(q_raw, query, 0)
-        load_rows(q_raw, query, 1)
         load_scales(nc.sync, val_bytes, vals_scales)
+        load_rows(q_raw, query, 1)
         nc.sync.dma_start(out=sharp_col[:], in_=sharp.rearrange("(p r) o -> p (r o)", r=PACK))
         nc.sync.dma_start(out=val_words[:].bitcast(I32), in_=vals_words[0].bitcast(I32))
         nc.sync.dma_start(out=lse_col[:], in_=lse.rearrange("o (p m) -> (o p) m", m=PACK))
@@ -78,13 +77,10 @@ def tile_attend_gsharpness_pl_kernel(tc, query, keys_words, keys_scales, sharp, 
             nc.vector.tensor_copy(picked[:], window[:].indirect(offsets[:]))
             return picked
 
-        def round_rows(name, raw):
-            grouped = sb(name, [P, PACK, P, PACK], BF16)
+        def round_rows(copy, grouped, raw, c):
             per = P // HALVES
-            for c in range(HALVES):
-                nc.scalar.copy(out=grouped[:, :, c * per:(c + 1) * per, :].rearrange("p m s j -> p s m j"),
-                               in_=raw[c][:].rearrange("p j (s m) -> p s m j", m=PACK))
-            return grouped
+            copy(out=grouped[:, :, c * per:(c + 1) * per, :].rearrange("p m s j -> p s m j"),
+                 in_=raw[c][:].rearrange("p j (s m) -> p s m j", m=PACK))
 
         def quantize(name, grouped):
             codes = sb(name + "_codes", [P, Q], U32)
@@ -98,21 +94,24 @@ def tile_attend_gsharpness_pl_kernel(tc, query, keys_words, keys_scales, sharp, 
 
         def product(name, rows, words, bytes_, m):
             codes, scales = rows
-            bank = psum.tile([P, I], F32, name=name, tag="product", bufs=7)
+            bank = psum.tile([P, I], F32, name=name, tag="product", bufs=6)
             cols = slice(m * P, (m + 1) * P)
             nc.tensor.matmul_mx(out=bank[:], lhsT=codes[:, cols].bitcast(FP8X4), lhsT_scale=scales[:, cols],
                                 rhs=words[:].bitcast(FP4X4), rhs_scale=bytes_[:], start=True, stop=True)
             return bank[:].rearrange("p (s r) -> p r s", r=PACK)
 
-        q_bf = round_rows("q_bf", q_raw)
+        q_bf = sb("q_bf", [P, PACK, P, PACK], BF16)
+        g_bf = sb("g_bf", [P, PACK, P, PACK], BF16)
+        round_rows(nc.scalar.copy, q_bf, q_raw, 0)
         k_words = gather("k_words", key_words, U16)
         k_bytes = gather("k_bytes", key_bytes, U8)
         v_bytes = gather("v_bytes", val_bytes, U8)
+        round_rows(nc.vector.tensor_copy, q_bf, q_raw, 1)
         q_mx = quantize("q", q_bf)
 
         neg_lse = sb("neg_lse", [P, PACK], F32)
         nc.scalar.activation(out=neg_lse[:], in_=lse_col[:], func=ACT.Copy, scale=-1.0)
-        spread = psum.tile([P, PACK, P], F32, name="spread", tag="turned", bufs=1)
+        spread = psum.tile([P, PACK, P], F32, name="spread", tag="turned", bufs=2)
         for r in range(PACK):
             nc.tensor.transpose(spread[:, r, :], sharp_col[:, r:r + 1].to_broadcast([P, P]), ident[:])
         sharp_row = sb("sharp_row", [P, PACK, P], F32)
@@ -120,39 +119,48 @@ def tile_attend_gsharpness_pl_kernel(tc, query, keys_words, keys_scales, sharp, 
 
         scores = [product("a%d" % m, q_mx, k_words, k_bytes, m) for m in range(PACK)]
         v_words = gather("v_words", val_words, U16)
-        g_bf = round_rows("g_bf", g_raw)
 
         weights = []
-        for m in range(PACK):
-            logit = sb("logit%d" % m, [P, PACK, P], F32)
-            nc.vector.tensor_tensor(out=logit[:], in0=scores[m], in1=sharp_row[:], op=ALU.mult)
-            weight = sb("weight%d" % m, [P, PACK, P], F32)
-            nc.scalar.activation(out=weight[:], in_=logit[:], func=ACT.Exp, bias=neg_lse[:, m:m + 1])
-            weights.append(weight)
+        for c in range(HALVES):
+            round_rows(nc.scalar.copy, g_bf, g_raw, c)
+            pair = keep.tile([P, 2, PACK, P], F32, name="weights%d" % c, tag="g_raw%d" % c, align_bytes=64)
+            for u in range(2):
+                m = 2 * c + u
+                logit = sb("logit%d" % m, [P, PACK, P], F32)
+                nc.vector.tensor_tensor(out=logit[:], in0=scores[m], in1=sharp_row[:], op=ALU.mult)
+                nc.scalar.activation(out=pair[:, u], in_=logit[:], func=ACT.Exp, bias=neg_lse[:, m:m + 1])
+                weights.append(pair[:, u])
 
         g_mx = quantize("g", g_bf)
         scored = []
         for m in range(PACK):
             both = sb("both%d" % m, [P, PACK, P], F32)
-            nc.vector.scalar_tensor_tensor(out=both[:], in0=scores[m], scalar=SCALE, in1=weights[m][:],
+            nc.vector.scalar_tensor_tensor(out=both[:], in0=scores[m], scalar=SCALE, in1=weights[m],
                                            op0=ALU.mult, op1=ALU.mult)
             scored.append(both)
 
-        summed = psum.tile([P, PACK, P], F32, name="summed", tag="turned", bufs=1)
+        summed = [psum.tile([P, 2, P], F32, name="summed%d" % u, tag="turned", bufs=2) for u in range(2)]
         for m in range(PACK):
             grad = product("dp%d" % m, g_mx, v_words, v_bytes, m)
             ds = sb("ds%d" % m, [P, PACK, P], F32)
-            nc.vector.scalar_tensor_tensor(out=ds[:], in0=grad, scalar=delta_col[:, m:m + 1], in1=scored[m][:],
-                                           op0=ALU.subtract, op1=ALU.mult)
-            for r in range(PACK):
-                nc.tensor.matmul(summed[:, r, :], lhsT=ds[:, r, :], rhs=ident[:], is_transpose=True,
-                                 start=(m == 0 and r == 0), stop=(m == PACK - 1 and r == PACK - 1))
+            step = 2 if m == PACK - 1 else PACK
+            for r0 in range(0, PACK, step):
+                rs = slice(r0, r0 + step)
+                nc.vector.scalar_tensor_tensor(out=ds[:, rs], in0=grad[:, rs], scalar=delta_col[:, m:m + 1],
+                                               in1=scored[m][:, rs], op0=ALU.subtract, op1=ALU.mult)
+                for r in range(r0, r0 + step):
+                    nc.tensor.matmul(summed[r // 2][:, r % 2, :], lhsT=ds[:, r, :], rhs=ident[:], is_transpose=True,
+                                     start=(m == 0 and r % 2 == 0), stop=(m == PACK - 1 and r % 2 == 1))
 
-        pairs = summed[:].rearrange("p r (g h) -> p h r g", h=2)
         partial = sb("partial", [P, PACK, G], F32)
-        nc.vector.tensor_tensor(out=partial[:], in0=pairs[:, 0], in1=old_sb[:], op=ALU.add)
         result = sb("result", [P, PACK, G], F32)
-        nc.vector.tensor_tensor(out=result[:], in0=pairs[:, 1], in1=partial[:], op=ALU.add)
+        pairs = [summed[u][:].rearrange("p r (g h) -> p h r g", h=2) for u in range(2)]
+        for u in range(2):
+            rs = slice(2 * u, 2 * u + 2)
+            nc.vector.tensor_tensor(out=partial[:, rs], in0=pairs[u][:, 0], in1=old_sb[:, rs], op=ALU.add)
+        for u in range(2):
+            rs = slice(2 * u, 2 * u + 2)
+            nc.vector.tensor_tensor(out=result[:, rs], in0=pairs[u][:, 1], in1=partial[:, rs], op=ALU.add)
         nc.sync.dma_start(out=out_0.rearrange("(p r) g -> p r g", r=PACK), in_=result[:])
 
         rounded = sb("rounded", [P, G, PACK], BF16)
@@ -163,6 +171,6 @@ def tile_attend_gsharpness_pl_kernel(tc, query, keys_words, keys_scales, sharp, 
                               in_=rounded[:].rearrange("p g r -> p (g r)"))
         nc.sync.dma_start(out=out_1[0].rearrange("p c t -> p (c t)").bitcast(I32), in_=out_codes[:].bitcast(I32))
         for quad in range(4):
-            queue = nc.scalar if quad % 2 == 0 else nc.sync
+            queue = nc.sync if quad == 3 else nc.scalar
             queue.dma_start(out=out_2[0, 4 * quad:4 * quad + 4, :].bitcast(I32),
                             in_=out_scales[32 * quad:32 * quad + 4, :].bitcast(I32))

@@ -30,50 +30,45 @@ def tile_attend_gsharpness_pl_kernel(tc, query, keys_words, keys_scales, sharp, 
         keep = ctx.enter_context(tc.tile_pool(name="keep", bufs=1))
         psum = ctx.enter_context(tc.psum_pool(name="psum", bufs=1))
 
-        def sb(name, shape, dtype):
-            return keep.tile(shape, dtype, name=name, align_bytes=64)
+        def sb(name, shape, dtype, after=None):
+            return keep.tile(shape, dtype, name=name, tag=after or name, align_bytes=64)
 
         offsets = sb("offsets", [P, I // 16], U16)
         key_words = sb("key_words", [P, T], U16)
-        val_words = sb("val_words", [P, T], U16)
         key_bytes = sb("key_bytes", [P, T], U8)
         val_bytes = sb("val_bytes", [P, T], U8)
         width = Q // HALVES
         q_raw = [sb("q_raw%d" % c, [P, PACK, width], F32) for c in range(HALVES)]
-        g_raw = [sb("g_raw%d" % c, [P, PACK, width], F32) for c in range(HALVES)]
         sharp_col = sb("sharp_col", [P, PACK], F32)
-        lse_col = sb("lse_col", [P, PACK], F32)
-        delta_col = sb("delta_col", [P, PACK], F32)
-        old_sb = sb("old_sb", [P, PACK, G], F32)
         ident = sb("ident", [P, P], F32)
 
+        key_plane = sb("key_plane", [P, I], U8)
         nc.vector.memset(key_bytes[:].bitcast(I32), 0)
-        nc.vector.memset(val_bytes[:].bitcast(I32), 0)
+        nc.gpsimd.memset(val_bytes[:].bitcast(I32), 0)
+        nc.vector.memset(key_plane[:].bitcast(I32), 0)
 
         def load_rows(dst, src, c):
             nc.sync.dma_start(out=dst[c][:], in_=src.rearrange("(p j) q -> p j q", j=PACK)[:, :, c * width:(c + 1) * width])
 
-        def load_scales(queue, dst, src):
+        def place_scales(queue, plane, picked):
             for row in range(4):
-                queue.dma_start(out=dst[row:P:32, :].bitcast(I32), in_=src[0, row:16:4, :].bitcast(I32))
+                queue.dma_start(out=plane[row:P:32, :].bitcast(I32), in_=picked[8 * row:P:32, :].bitcast(I32))
 
         make_identity(nc, ident[:])
         nc.sync.dma_start(offsets[:], offs)
-        nc.sync.dma_start(out=key_words[:].bitcast(I32), in_=keys_words[0].bitcast(I32))
-        load_scales(nc.sync, key_bytes, keys_scales)
         load_rows(q_raw, query, 0)
-        load_scales(nc.sync, val_bytes, vals_scales)
-        load_rows(q_raw, query, 1)
+        nc.sync.dma_start(out=key_bytes[0:P:8, :].bitcast(I32), in_=keys_scales[0].bitcast(I32))
+        nc.sync.dma_start(out=val_bytes[0:P:8, :].bitcast(I32), in_=vals_scales[0].bitcast(I32))
+        nc.sync.dma_start(out=key_words[:].bitcast(I32), in_=keys_words[0].bitcast(I32))
         nc.sync.dma_start(out=sharp_col[:], in_=sharp.rearrange("(p r) o -> p (r o)", r=PACK))
+        load_rows(q_raw, query, 1)
+        val_words = sb("val_words", [P, T], U16)
         nc.sync.dma_start(out=val_words[:].bitcast(I32), in_=vals_words[0].bitcast(I32))
-        nc.sync.dma_start(out=lse_col[:], in_=lse.rearrange("o (p m) -> (o p) m", m=PACK))
-        load_rows(g_raw, gout, 0)
-        load_rows(g_raw, gout, 1)
-        nc.sync.dma_start(out=delta_col[:], in_=delta.rearrange("o (p m) -> (o p) m", m=PACK))
-        nc.sync.dma_start(out=old_sb[:], in_=old.rearrange("(p r) g -> p r g", r=PACK))
+        lse_col = sb("lse_col", [P, PACK], F32)
+        nc.gpsimd.dma_start(out=lse_col[:], in_=lse.rearrange("o (p m) -> (o p) m", m=PACK))
 
-        def gather(name, window, dtype):
-            picked = sb(name, [P, I], dtype)
+        def gather(name, window, dtype, after=None):
+            picked = sb(name, [P, I], dtype, after=after)
             nc.vector.tensor_copy(picked[:], window[:].indirect(offsets[:]))
             return picked
 
@@ -86,10 +81,7 @@ def tile_attend_gsharpness_pl_kernel(tc, query, keys_words, keys_scales, sharp, 
             codes = sb(name + "_codes", [P, Q], U32)
             scales = sb(name + "_scales", [P, Q], U8)
             flat = grouped[:].rearrange("p m s j -> p (m s j)")
-            for c in range(2):
-                cols = slice(c * 256, (c + 1) * 256)
-                nc.vector.quantize_mx(out=codes[:, cols].bitcast(FP8X4), scales=scales[:, cols],
-                                      in_=flat[:, c * 1024:(c + 1) * 1024])
+            nc.vector.quantize_mx(out=codes[:].bitcast(FP8X4), scales=scales[:], in_=flat)
             return codes, scales
 
         def product(name, rows, words, bytes_, m):
@@ -102,52 +94,62 @@ def tile_attend_gsharpness_pl_kernel(tc, query, keys_words, keys_scales, sharp, 
 
         q_bf = sb("q_bf", [P, PACK, P, PACK], BF16)
         g_bf = sb("g_bf", [P, PACK, P, PACK], BF16)
-        round_rows(nc.scalar.copy, q_bf, q_raw, 0)
-        k_words = gather("k_words", key_words, U16)
         k_bytes = gather("k_bytes", key_bytes, U8)
+        place_scales(nc.sync, key_plane, k_bytes)
         v_bytes = gather("v_bytes", val_bytes, U8)
-        round_rows(nc.vector.tensor_copy, q_bf, q_raw, 1)
+        k_words = gather("k_words", key_words, U16)
+        round_rows(nc.scalar.copy, q_bf, q_raw, 0)
+        round_rows(nc.scalar.copy, q_bf, q_raw, 1)
+        g_homes = ["key_bytes", "val_bytes"]
+        g_raw = [sb("g_raw%d" % c, [P, PACK, width], F32, after=g_homes[c]) for c in range(HALVES)]
+        load_rows(g_raw, gout, 0)
+        load_rows(g_raw, gout, 1)
         q_mx = quantize("q", q_bf)
+        val_plane = sb("val_plane", [P, I], U8, after="key_words")
+        nc.gpsimd.memset(val_plane[:].bitcast(I32), 0)
+        place_scales(nc.sync, val_plane, v_bytes)
 
-        neg_lse = sb("neg_lse", [P, PACK], F32)
-        nc.scalar.activation(out=neg_lse[:], in_=lse_col[:], func=ACT.Copy, scale=-1.0)
         spread = psum.tile([P, PACK, P], F32, name="spread", tag="turned", bufs=2)
         for r in range(PACK):
             nc.tensor.transpose(spread[:, r, :], sharp_col[:, r:r + 1].to_broadcast([P, P]), ident[:])
         sharp_row = sb("sharp_row", [P, PACK, P], F32)
         nc.scalar.copy(out=sharp_row[:], in_=spread[:])
+        neg_lse = sb("neg_lse", [P, PACK], F32)
+        nc.gpsimd.tensor_scalar(out=neg_lse[:], in0=lse_col[:], scalar1=-1.0, scalar2=None, op0=ALU.mult)
 
-        scores = [product("a%d" % m, q_mx, k_words, k_bytes, m) for m in range(PACK)]
-        v_words = gather("v_words", val_words, U16)
+        scores = [product("a%d" % m, q_mx, k_words, key_plane, m) for m in range(PACK)]
+        v_words = gather("v_words", val_words, U16, after="q_bf")
+        delta_col = sb("delta_col", [P, PACK], F32, after="q_scales")
+        nc.sync.dma_start(out=delta_col[:], in_=delta.rearrange("o (p m) -> (o p) m", m=PACK))
+        old_sb = sb("old_sb", [P, PACK, G], F32, after="q_codes")
+        nc.sync.dma_start(out=old_sb[:], in_=old.rearrange("(p r) g -> p r g", r=PACK))
+        logits = sb("logits", [P, PACK, PACK, P], F32, after="val_words")
 
         weights = []
         for c in range(HALVES):
             round_rows(nc.scalar.copy, g_bf, g_raw, c)
-            pair = keep.tile([P, 2, PACK, P], F32, name="weights%d" % c, tag="g_raw%d" % c, align_bytes=64)
+            pair = sb("weights%d" % c, [P, 2, PACK, P], F32, after=g_homes[c])
             for u in range(2):
                 m = 2 * c + u
-                logit = sb("logit%d" % m, [P, PACK, P], F32)
-                nc.vector.tensor_tensor(out=logit[:], in0=scores[m], in1=sharp_row[:], op=ALU.mult)
-                nc.scalar.activation(out=pair[:, u], in_=logit[:], func=ACT.Exp, bias=neg_lse[:, m:m + 1])
+                nc.vector.tensor_tensor(out=logits[:, m], in0=scores[m], in1=sharp_row[:], op=ALU.mult)
+                nc.scalar.activation(out=pair[:, u], in_=logits[:, m], func=ACT.Exp, bias=neg_lse[:, m:m + 1])
                 weights.append(pair[:, u])
 
         g_mx = quantize("g", g_bf)
-        scored = []
+        scored = sb("scored", [P, PACK, PACK, P], F32, after="sharp_row")
         for m in range(PACK):
-            both = sb("both%d" % m, [P, PACK, P], F32)
-            nc.vector.scalar_tensor_tensor(out=both[:], in0=scores[m], scalar=SCALE, in1=weights[m],
+            nc.vector.scalar_tensor_tensor(out=scored[:, m], in0=scores[m], scalar=SCALE, in1=weights[m],
                                            op0=ALU.mult, op1=ALU.mult)
-            scored.append(both)
 
         summed = [psum.tile([P, 2, P], F32, name="summed%d" % u, tag="turned", bufs=2) for u in range(2)]
         for m in range(PACK):
-            grad = product("dp%d" % m, g_mx, v_words, v_bytes, m)
+            grad = product("dp%d" % m, g_mx, v_words, val_plane, m)
             ds = sb("ds%d" % m, [P, PACK, P], F32)
             step = 2 if m == PACK - 1 else PACK
             for r0 in range(0, PACK, step):
                 rs = slice(r0, r0 + step)
                 nc.vector.scalar_tensor_tensor(out=ds[:, rs], in0=grad[:, rs], scalar=delta_col[:, m:m + 1],
-                                               in1=scored[m][:, rs], op0=ALU.subtract, op1=ALU.mult)
+                                               in1=scored[:, m, rs], op0=ALU.subtract, op1=ALU.mult)
                 for r in range(r0, r0 + step):
                     nc.tensor.matmul(summed[r // 2][:, r % 2, :], lhsT=ds[:, r, :], rhs=ident[:], is_transpose=True,
                                      start=(m == 0 and r % 2 == 0), stop=(m == PACK - 1 and r % 2 == 1))

@@ -77,8 +77,8 @@ def tile_attend_gsharpness_pl_kernel(tc, query, keys_words, keys_scales, sharp, 
             copy(out=grouped[:, :, c * per:(c + 1) * per, :].rearrange("p m s j -> p s m j"),
                  in_=raw[c][:].rearrange("p j (s m) -> p s m j", m=PACK))
 
-        def quantize(name, grouped):
-            codes = sb(name + "_codes", [P, Q], U32)
+        def quantize(name, grouped, after=None):
+            codes = sb(name + "_codes", [P, Q], U32, after=after)
             scales = sb(name + "_scales", [P, Q], U8)
             flat = grouped[:].rearrange("p m s j -> p (m s j)")
             nc.vector.quantize_mx(out=codes[:].bitcast(FP8X4), scales=scales[:], in_=flat)
@@ -117,29 +117,34 @@ def tile_attend_gsharpness_pl_kernel(tc, query, keys_words, keys_scales, sharp, 
         neg_lse = sb("neg_lse", [P, PACK], F32)
         nc.gpsimd.tensor_scalar(out=neg_lse[:], in0=lse_col[:], scalar1=-1.0, scalar2=None, op0=ALU.mult)
 
-        scores = [product("a%d" % m, q_mx, k_words, key_plane, m) for m in range(PACK)]
+        last = PACK - 1
+        scores = {m: product("a%d" % m, q_mx, k_words, key_plane, m) for m in [0, last] + list(range(1, last))}
         v_words = gather("v_words", val_words, U16, after="q_bf")
         delta_col = sb("delta_col", [P, PACK], F32, after="q_scales")
         nc.sync.dma_start(out=delta_col[:], in_=delta.rearrange("o (p m) -> (o p) m", m=PACK))
-        old_sb = sb("old_sb", [P, PACK, G], F32, after="q_codes")
+        old_sb = sb("old_sb", [P, PACK, G], F32, after="k_bytes")
         nc.sync.dma_start(out=old_sb[:], in_=old.rearrange("(p r) g -> p r g", r=PACK))
-        logits = sb("logits", [P, PACK, PACK, P], F32, after="val_words")
+        logits = sb("logits", [P, PACK - 1, PACK, P], F32, after="val_words")
 
-        weights = []
-        for c in range(HALVES):
-            round_rows(nc.scalar.copy, g_bf, g_raw, c)
-            pair = sb("weights%d" % c, [P, 2, PACK, P], F32, after=g_homes[c])
-            for u in range(2):
-                m = 2 * c + u
-                nc.vector.tensor_tensor(out=logits[:, m], in0=scores[m], in1=sharp_row[:], op=ALU.mult)
-                nc.scalar.activation(out=pair[:, u], in_=logits[:, m], func=ACT.Exp, bias=neg_lse[:, m:m + 1])
-                weights.append(pair[:, u])
+        round_rows(nc.scalar.copy, g_bf, g_raw, 0)
+        scaled = sb("scaled", [P, PACK, P], F32, after=g_homes[0])
+        nc.scalar.activation(out=scaled[:], in_=scores[last], func=ACT.Copy, scale=SCALE)
+        scaled_logit = sb("scaled_logit", [P, PACK, P], F32)
+        nc.gpsimd.tensor_tensor(out=scaled_logit[:], in0=scaled[:], in1=sharp_row[:], op=ALU.mult)
+        round_rows(nc.scalar.copy, g_bf, g_raw, 1)
+        weights = sb("weights", [P, PACK, PACK, P], F32, after=g_homes[1])
+        for m in range(last):
+            nc.vector.tensor_tensor(out=logits[:, m], in0=scores[m], in1=sharp_row[:], op=ALU.mult)
+            nc.scalar.activation(out=weights[:, m], in_=logits[:, m], func=ACT.Exp, bias=neg_lse[:, m:m + 1])
+        nc.scalar.activation(out=weights[:, last], in_=scaled_logit[:], func=ACT.Exp, bias=neg_lse[:, last:last + 1],
+                             scale=1.0 / SCALE)
 
-        g_mx = quantize("g", g_bf)
-        scored = sb("scored", [P, PACK, PACK, P], F32, after="sharp_row")
-        for m in range(PACK):
-            nc.vector.scalar_tensor_tensor(out=scored[:, m], in0=scores[m], scalar=SCALE, in1=weights[m],
+        g_mx = quantize("g", g_bf, after="q_codes")
+        scored = sb("scored", [P, PACK, PACK, P], F32, after="g_bf")
+        for m in range(last):
+            nc.vector.scalar_tensor_tensor(out=scored[:, m], in0=scores[m], scalar=SCALE, in1=weights[:, m],
                                            op0=ALU.mult, op1=ALU.mult)
+        nc.gpsimd.tensor_tensor(out=scored[:, last], in0=scaled[:], in1=weights[:, last], op=ALU.mult)
 
         summed = [psum.tile([P, 2, P], F32, name="summed%d" % u, tag="turned", bufs=2) for u in range(2)]
         for m in range(PACK):

from contextlib import ExitStack

import concourse.mybir as mybir
from concourse.masks import make_identity

D, E, T, I, Q, G = 512, 512, 2048, 512, 512, 64
FLOPS = 2 * I * Q * (D + E)

F32 = mybir.dt.float32
BF16 = mybir.dt.bfloat16
I32 = mybir.dt.int32
U32 = mybir.dt.uint32
U16 = mybir.dt.uint16
U8 = mybir.dt.uint8
FP8X4 = mybir.dt.float8_e4m3fn_x4
FP4X4 = mybir.dt.float4_e2m1fn_x4
ALU = mybir.AluOpType
ACT = mybir.ActivationFunctionType

P = 128
PACK = 4
HALVES = 2
SCALE = 512.0


def tile_attend_gsharpness_pl_kernel(tc, query, keys_words, keys_scales, sharp, lse, gout, vals_words,
                                      vals_scales, delta, old, offs, out_0, out_1, out_2):
    nc = tc.nc
    with ExitStack() as ctx:
        keep = ctx.enter_context(tc.tile_pool(name="keep", bufs=1))
        psum = ctx.enter_context(tc.psum_pool(name="psum", bufs=1))

        def sb(name, shape, dtype, after=None):
            return keep.tile(shape, dtype, name=name, tag=after or name, align_bytes=64)

        offsets = sb("offsets", [P, I // 16], U16)
        key_words = sb("key_words", [P, T], U16)
        key_bytes = sb("key_bytes", [P, T], U8)
        val_bytes = sb("val_bytes", [P, T], U8)
        width = Q // HALVES
        q_raw = [sb("q_raw%d" % c, [P, PACK, width], F32) for c in range(HALVES)]
        sharp_col = sb("sharp_col", [P, PACK], F32)
        ident = sb("ident", [P, P], F32)

        key_plane = sb("key_plane", [P, I], U8)
        nc.vector.memset(key_bytes[:].bitcast(I32), 0)
        nc.gpsimd.memset(val_bytes[:].bitcast(I32), 0)
        nc.vector.memset(key_plane[:].bitcast(I32), 0)

        def load_rows(dst, src, c):
            nc.sync.dma_start(out=dst[c][:], in_=src.rearrange("(p j) q -> p j q", j=PACK)[:, :, c * width:(c + 1) * width])

        def place_scales(queue, plane, picked):
            for row in range(4):
                queue.dma_start(out=plane[row:P:32, :].bitcast(I32), in_=picked[8 * row:P:32, :].bitcast(I32))

        make_identity(nc, ident[:])
        nc.sync.dma_start(offsets[:], offs)
        load_rows(q_raw, query, 0)
        nc.sync.dma_start(out=key_bytes[0:P:8, :].bitcast(I32), in_=keys_scales[0].bitcast(I32))
        nc.sync.dma_start(out=val_bytes[0:P:8, :].bitcast(I32), in_=vals_scales[0].bitcast(I32))
        nc.sync.dma_start(out=key_words[:].bitcast(I32), in_=keys_words[0].bitcast(I32))
        nc.sync.dma_start(out=sharp_col[:], in_=sharp.rearrange("(p r) o -> p (r o)", r=PACK))
        load_rows(q_raw, query, 1)
        val_words = sb("val_words", [P, T], U16)
        nc.sync.dma_start(out=val_words[:].bitcast(I32), in_=vals_words[0].bitcast(I32))
        lse_col = sb("lse_col", [P, PACK], F32)
        nc.gpsimd.dma_start(out=lse_col[:], in_=lse.rearrange("o (p m) -> (o p) m", m=PACK))

        def gather(name, window, dtype, after=None):
            picked = sb(name, [P, I], dtype, after=after)
            nc.vector.tensor_copy(picked[:], window[:].indirect(offsets[:]))
            return picked

        def round_rows(copy, grouped, raw, c):
            per = P // HALVES
            copy(out=grouped[:, :, c * per:(c + 1) * per, :].rearrange("p m s j -> p s m j"),
                 in_=raw[c][:].rearrange("p j (s m) -> p s m j", m=PACK))

        def quantize(name, grouped, after=None):
            codes = sb(name + "_codes", [P, Q], U32, after=after)
            scales = sb(name + "_scales", [P, Q], U8)
            flat = grouped[:].rearrange("p m s j -> p (m s j)")
            nc.vector.quantize_mx(out=codes[:].bitcast(FP8X4), scales=scales[:], in_=flat)
            return codes, scales

        def product(name, rows, words, bytes_, m):
            codes, scales = rows
            bank = psum.tile([P, I], F32, name=name, tag="product", bufs=6)
            cols = slice(m * P, (m + 1) * P)
            nc.tensor.matmul_mx(out=bank[:], lhsT=codes[:, cols].bitcast(FP8X4), lhsT_scale=scales[:, cols],
                                rhs=words[:].bitcast(FP4X4), rhs_scale=bytes_[:], start=True, stop=True)
            return bank[:].rearrange("p (s r) -> p r s", r=PACK)

        q_bf = sb("q_bf", [P, PACK, P, PACK], BF16)
        g_bf = sb("g_bf", [P, PACK, P, PACK], BF16)
        k_bytes = gather("k_bytes", key_bytes, U8)
        place_scales(nc.sync, key_plane, k_bytes)
        v_bytes = gather("v_bytes", val_bytes, U8)
        k_words = gather("k_words", key_words, U16)
        round_rows(nc.scalar.copy, q_bf, q_raw, 0)
        round_rows(nc.scalar.copy, q_bf, q_raw, 1)
        g_homes = ["key_bytes", "val_bytes"]
        g_raw = [sb("g_raw%d" % c, [P, PACK, width], F32, after=g_homes[c]) for c in range(HALVES)]
        load_rows(g_raw, gout, 0)
        load_rows(g_raw, gout, 1)
        q_mx = quantize("q", q_bf)
        val_plane = sb("val_plane", [P, I], U8, after="key_words")
        nc.gpsimd.memset(val_plane[:].bitcast(I32), 0)
        place_scales(nc.sync, val_plane, v_bytes)

        spread = psum.tile([P, PACK, P], F32, name="spread", tag="turned", bufs=2)
        for r in range(PACK):
            nc.tensor.transpose(spread[:, r, :], sharp_col[:, r:r + 1].to_broadcast([P, P]), ident[:])
        sharp_row = sb("sharp_row", [P, PACK, P], F32)
        nc.scalar.copy(out=sharp_row[:], in_=spread[:])
        neg_lse = sb("neg_lse", [P, PACK], F32)
        nc.gpsimd.tensor_scalar(out=neg_lse[:], in0=lse_col[:], scalar1=-1.0, scalar2=None, op0=ALU.mult)

        last = PACK - 1
        scores = {m: product("a%d" % m, q_mx, k_words, key_plane, m) for m in [0, last] + list(range(1, last))}
        v_words = gather("v_words", val_words, U16, after="q_bf")
        delta_col = sb("delta_col", [P, PACK], F32, after="q_scales")
        nc.sync.dma_start(out=delta_col[:], in_=delta.rearrange("o (p m) -> (o p) m", m=PACK))
        old_sb = sb("old_sb", [P, PACK, G], F32, after="k_bytes")
        nc.sync.dma_start(out=old_sb[:], in_=old.rearrange("(p r) g -> p r g", r=PACK))
        logits = sb("logits", [P, PACK - 1, PACK, P], F32, after="val_words")

        round_rows(nc.scalar.copy, g_bf, g_raw, 0)
        scaled = sb("scaled", [P, PACK, P], F32, after=g_homes[0])
        nc.scalar.activation(out=scaled[:], in_=scores[last], func=ACT.Copy, scale=SCALE)
        scaled_logit = sb("scaled_logit", [P, PACK, P], F32)
        nc.gpsimd.tensor_tensor(out=scaled_logit[:], in0=scaled[:], in1=sharp_row[:], op=ALU.mult)
        round_rows(nc.scalar.copy, g_bf, g_raw, 1)
        weights = sb("weights", [P, PACK, PACK, P], F32, after=g_homes[1])
        for m in range(last):
            nc.vector.tensor_tensor(out=logits[:, m], in0=scores[m], in1=sharp_row[:], op=ALU.mult)
            nc.scalar.activation(out=weights[:, m], in_=logits[:, m], func=ACT.Exp, bias=neg_lse[:, m:m + 1])
        nc.scalar.activation(out=weights[:, last], in_=scaled_logit[:], func=ACT.Exp, bias=neg_lse[:, last:last + 1],
                             scale=1.0 / SCALE)

        g_mx = quantize("g", g_bf, after="q_codes")
        scored = sb("scored", [P, PACK, PACK, P], F32, after="g_bf")
        for m in range(last):
            nc.vector.scalar_tensor_tensor(out=scored[:, m], in0=scores[m], scalar=SCALE, in1=weights[:, m],
                                           op0=ALU.mult, op1=ALU.mult)
        nc.gpsimd.tensor_tensor(out=scored[:, last], in0=scaled[:], in1=weights[:, last], op=ALU.mult)

        summed = [psum.tile([P, 2, P], F32, name="summed%d" % u, tag="turned", bufs=2) for u in range(2)]
        for m in range(PACK):
            grad = product("dp%d" % m, g_mx, v_words, val_plane, m)
            ds = sb("ds%d" % m, [P, PACK, P], F32)
            step = 2 if m == PACK - 1 else PACK
            for r0 in range(0, PACK, step):
                rs = slice(r0, r0 + step)
                nc.vector.scalar_tensor_tensor(out=ds[:, rs], in0=grad[:, rs], scalar=delta_col[:, m:m + 1],
                                               in1=scored[:, m, rs], op0=ALU.subtract, op1=ALU.mult)
                for r in range(r0, r0 + step):
                    nc.tensor.matmul(summed[r // 2][:, r % 2, :], lhsT=ds[:, r, :], rhs=ident[:], is_transpose=True,
                                     start=(m == 0 and r % 2 == 0), stop=(m == PACK - 1 and r % 2 == 1))

        partial = sb("partial", [P, PACK, G], F32)
        result = sb("result", [P, PACK, G], F32)
        pairs = [summed[u][:].rearrange("p r (g h) -> p h r g", h=2) for u in range(2)]
        for u in range(2):
            rs = slice(2 * u, 2 * u + 2)
            nc.vector.tensor_tensor(out=partial[:, rs], in0=pairs[u][:, 0], in1=old_sb[:, rs], op=ALU.add)
        for u in range(2):
            rs = slice(2 * u, 2 * u + 2)
            nc.vector.tensor_tensor(out=result[:, rs], in0=pairs[u][:, 1], in1=partial[:, rs], op=ALU.add)
        nc.sync.dma_start(out=out_0.rearrange("(p r) g -> p r g", r=PACK), in_=result[:])

        rounded = sb("rounded", [P, G, PACK], BF16)
        nc.vector.tensor_copy(out=rounded[:], in_=result[:].rearrange("p r g -> p g r"))
        out_codes = sb("out_codes", [P, G], U32)
        out_scales = sb("out_scales", [P, G], U8)
        nc.vector.quantize_mx(out=out_codes[:].bitcast(FP8X4), scales=out_scales[:],
                              in_=rounded[:].rearrange("p g r -> p (g r)"))
        nc.sync.dma_start(out=out_1[0].rearrange("p c t -> p (c t)").bitcast(I32), in_=out_codes[:].bitcast(I32))
        for quad in range(4):
            queue = nc.sync if quad == 3 else nc.scalar
            queue.dma_start(out=out_2[0, 4 * quad:4 * quad + 4, :].bitcast(I32),
                            in_=out_scales[32 * quad:32 * quad + 4, :].bitcast(I32))
